import numpy as np, ml_dtypes
CORES = [2,10,50,58,66,74,122]
N = 7
import mx_ref
NC, G = 192, 4
C = np.float32(0.043)
WID = [192,192,160,128,128,160,192]
BF = ml_dtypes.bfloat16
def cut(t, i, w=512):
    return t[:, w * i:w * i + w]
def tile(rs):
    return np.stack(rs, axis=2).reshape(128, -1).astype(BF)
def layer(w, X):
    out = []
    for i in range(G):
        for t in range(len(X)):
            p = mx_ref.matmul(mx_ref.quantize(cut(w, len(X) * i + t)), X[t])
            z = p if t == 0 else z + p
        out.append(z)
    return out
def act(Z):
    return [np.maximum(z, 0) * C for z in Z]
def setup_inputs(rng):
    def f(*shape):
        return mx_ref.flush((rng.standard_normal(shape, dtype=np.float32) * np.exp2(rng.integers(-2, 3, shape[:-1] + (1,)))).astype(BF))
    return {"x": f(N, 128, 4 * NC), "w1": f(N, 128, G * 512), "w2": f(N, 128, 512)}
def setup_inputs_blocks(rng):
    d = setup_inputs(rng)
    for k in ("x", "w1", "w2"): d[k] = mx_ref.spread(d[k], rng, 2)
    return d
def setup_inputs_wide(rng):
    d = setup_inputs(rng)
    for k in ("x", "w1", "w2"): d[k] = mx_ref.flush((d[k].astype(np.float32) * np.exp2(rng.integers(-6, 7, (N, 1, 1))).astype(np.float32)).astype(BF))
    return d
def reference(x, w1, w2):
    X = [mx_ref.quantize(x[j][:, :4 * WID[j]]) for j in range(N)]
    y = np.full((N, 128, NC), np.nan, np.float32)
    for c in range(N):
        for r in range(N):
            p = mx_ref.matmul(mx_ref.quantize(w2[r]), mx_ref.quantize(tile(act(layer(w1[r], [X[c]])))))
            z = p if r == 0 else z + p
        y[c][:, :WID[c]] = z
    return {"y": y}

@@ -1,0 +1,141 @@
+from concourse.bass import DstId, RemoteDMATransfer
+from concourse.mybir import dt, AluOpType, ActivationFunctionType
+
+NR = 7
+TOT = 1152
+OPT = {}
+
+SCRATCH = {
+    "xb": ("sbuf", [128, 768], "bfloat16"),
+    "w1b": ("sbuf", [128, 2048], "bfloat16"),
+    "w2b": ("sbuf", [128, 512], "bfloat16"),
+    "xq": ("sbuf", [128, TOT], "float8_e4m3fn_x4"),
+    "xs": ("sbuf", [128, TOT], "uint8"),
+    "wq": ("sbuf", [128, 640], "float8_e4m3fn_x4"),
+    "ws": ("sbuf", [128, 640], "uint8"),
+    "h": ("sbuf", [128, 4 * TOT], "bfloat16"),
+    "hq": ("sbuf", [128, TOT], "float8_e4m3fn_x4"),
+    "hs": ("sbuf", [128, TOT], "uint8"),
+    "yo": ("sbuf", [128, TOT], "float32"),
+    "yl": ("sbuf", [128, NR * 192], "float32"),
+    "acc": ("sbuf", [128, 192], "float32"),
+    "pz": ("psum", [128, 512 * 6], "float32"),
+    "py": ("psum", [128, 512 * 2], "float32"),
+}
+SEMAPHORES = (["lx", "lw0", "lw1", "lw2", "lw3", "lw4", "qx", "qw", "z", "rs", "rv", "qh", "ym", "ev", "sent", "ac", "st"]
+              + ["x%d" % c for c in range(NR)] + ["y%d" % r for r in range(NR)])
+
+
+def bits(m):
+    return bin(m).count("1")
+
+
+def rank_program(g, core, T, topo):
+    me = T.rank_of(core)
+    if me is None:
+        return
+    cores = list(T.cores)
+    wid = T.tables["WID"]
+    off = [sum(wid[:c]) for c in range(NR)]
+
+    def targets(c):
+        rot = [(c + i) % NR for i in range(1, NR)]
+        mate = [r for r in rot if topo.mates(topo.chip(cores[c]), topo.chip(cores[r]))]
+        return mate + [r for r in rot if r not in mate]
+
+    def work(r):
+        return [r] + sorted([c for c in range(NR) if c != r], key=lambda c: (targets(c).index(r), (r - c) % NR))
+    order = work(me)
+    W = wid[me]
+    S, V, E = g.scalar, g.vector, g.tensor
+    sent = [0]
+
+    def send(out, src, sem, d):
+        rid, pid, _ = topo.addr(d)
+        m = topo.mask(core, d)
+        g.remote_dma(out, src, sem, T.sem.sent, pid, rid, m)
+        sent[0] += bits(m)
+    g.sync.dma_start(T.xb[:, :4 * W], T.x[:, :4 * W]).then_inc(T.sem.lx, 16)
+    for i in range(4):
+        g.sync.dma_start(T.w1b[:, 512 * i:512 * i + 512], T.w1[:, 512 * i:512 * i + 512]).then_inc(T.sem["lw%d" % i], 16)
+    g.sync.dma_start(T.w2b[:], T.w2[:]).then_inc(T.sem.lw4, 16)
+    a, b = off[me], off[me] + W
+    V.wait_ge(T.sem.lx, 16)
+    V.quantize_mx(T.xq[:, a:b], T.xs[:, a:b], T.xb[:, :4 * W]).then_inc(T.sem.qx, 1)
+    for i in range(5):
+        V.wait_ge(T.sem["lw%d" % i], 16)
+        src = T.w1b[:, 512 * i:512 * i + 512] if i < 4 else T.w2b[:]
+        V.quantize_mx(T.wq[:, 128 * i:128 * i + 128], T.ws[:, 128 * i:128 * i + 128], src).then_inc(T.sem.qw, 1)
+    g.wait_ge(T.sem.qx, 1)
+    codes, plane = T.xq[:, a:b].bitcast(dt.uint8), T.xs[:, a:b]
+    for r in targets(me):
+        send(codes, codes, T.sem["x%d" % me], cores[r])
+        send(plane, plane, T.sem["x%d" % me], cores[r])
+
+    vb, sb, ring = (1, 3), (0, 2), 6
+
+    def left(m):
+        return (T.sem.rv if m % 4 in vb else T.sem.rs), m // 4 * 2 + m % 4 // 2 + 1
+
+    def first(k):
+        c = order[k]
+        n, a = wid[c], off[c]
+        if c == me:
+            E.wait_ge(T.sem.qx, 1)
+        else:
+            E.wait_ge(T.sem["x%d" % c], 2 * bits(topo.mask(cores[c], core)))
+        for b in range(4):
+            m = 4 * k + b
+            if k == 0:
+                E.wait_ge(T.sem.qw, b + 1)
+            if m >= ring:
+                E.wait_ge(*left(m - ring))
+            p = 512 * (m % ring)
+            E.matmul_mx(T.pz[:, p:p + n], T.wq[:, 128 * b:128 * b + 128], T.ws[:, 128 * b:128 * b + 128],
+                        T.xq[:, a:a + n], T.xs[:, a:a + n], True, True).then_inc(T.sem.z, 1)
+            out = T.h[:, 4 * a + b:4 * (a + n):4]
+            if b in vb:
+                V.wait_ge(T.sem.z, m + 1)
+                V.tensor_scalar(out, T.pz[:, p:p + n], 0.0, 0.043, AluOpType.max, AluOpType.mult).then_inc(T.sem.rv, 1)
+            else:
+                S.wait_ge(T.sem.z, m + 1)
+                S.activation(out, T.pz[:, p:p + n], ActivationFunctionType.Relu, scale=0.043).then_inc(T.sem.rs, 1)
+        V.wait_ge(T.sem.rs, 2 * (k + 1))
+        V.wait_ge(T.sem.rv, 2 * (k + 1))
+        V.quantize_mx(T.hq[:, a:a + n], T.hs[:, a:a + n], T.h[:, 4 * a:4 * (a + n)]).then_inc(T.sem.qh, 1)
+
+    def second(k):
+        c = order[k]
+        n, a = wid[c], off[c]
+        if k == 0:
+            E.wait_ge(T.sem.qw, 5)
+        E.wait_ge(T.sem.qh, k + 1)
+        if k >= 2:
+            E.wait_ge(T.sem.ev, k - 1)
+        p = 512 * (k % 2)
+        E.matmul_mx(T.py[:, p:p + n], T.wq[:, 512:640], T.ws[:, 512:640], T.hq[:, a:a + n], T.hs[:, a:a + n],
+                    True, True).then_inc(T.sem.ym, 1)
+        S.wait_ge(T.sem.ym, k + 1)
+        S.activation(T.yo[:, a:a + n], T.py[:, p:p + n], ActivationFunctionType.Copy).then_inc(T.sem.ev, 1)
+        if c != me:
+            g.wait_ge(T.sem.ev, k + 1)
+            send(T.yl[:, 192 * me:192 * me + n], T.yo[:, a:a + n], T.sem["y%d" % me], cores[c])
+
+    first(0)
+    for k in range(1, NR):
+        first(k)
+        second(k - 1)
+    second(NR - 1)
+    V.wait_ge(T.sem.ev, 1)
+    senders = sorted([r for r in range(NR) if r != me], key=lambda r: (work(r).index(me), (r - me) % NR))
+    prev = T.yo[:, a:a + W]
+    for i, r in enumerate(senders):
+        V.wait_ge(T.sem["y%d" % r], bits(topo.mask(cores[r], core)))
+        if i:
+            V.wait_ge(T.sem.ac, i)
+        V.tensor_tensor(T.acc[:, :W], prev, T.yl[:, 192 * r:192 * r + W], AluOpType.add).then_inc(T.sem.ac, 1)
+        prev = T.acc[:, :W]
+    g.sync.wait_ge(T.sem.ac, len(senders))
+    g.sync.dma_start(T.y[:, :W], T.acc[:, :W]).then_inc(T.sem.st, 16)
+    g.sync.wait_ge(T.sem.st, 16)
+    g.wait_ge(T.sem.sent, sent[0])

@@ -3,6 +3,7 @@ from concourse.mybir import dt, AluOpType, ActivationFunctionType
 
 NR = 7
 TOT = 1152
+CFG = {"nd": 4, "nh": 1, "hpos": 1, "ownpos": 0, "np": ()}
 OPT = {}
 
 SCRATCH = {
@@ -31,30 +32,56 @@ def bits(m):
 
 
 def rank_program(g, core, T, topo):
+    O = dict(CFG)
+    O.update(OPT)
     me = T.rank_of(core)
-    if me is None:
-        return
     cores = list(T.cores)
     wid = T.tables["WID"]
     off = [sum(wid[:c]) for c in range(NR)]
 
-    def targets(c):
+    def plan(c):
+        s = cores[c]
         rot = [(c + i) % NR for i in range(1, NR)]
-        mate = [r for r in rot if topo.mates(topo.chip(cores[c]), topo.chip(cores[r]))]
-        return mate + [r for r in rot if r not in mate]
+        dd, hh = rot[:O["nd"]], rot[O["nd"]:]
+        ok = [k for k in range(128) if k != s and topo.chip(k) == topo.chip(s) and all(topo.may_write(k, cores[r]) for r in rot)]
+        hs = [k for k in ok if topo.die(k) != topo.die(s)][:O["nh"]]
+        out, on = topo.mask(s, cores[rot[0]]), topo.mask(s, ok[0])
+        return dd, [(h, hh[j::len(hs)]) for j, h in enumerate(hs)], on & ~out
+    plans = [plan(c) for c in range(NR)]
+    helps = [(c, ds) for c in range(NR) for h, ds in plans[c][1] if h == core]
+    if me is None and not helps:
+        return
+
+    def step(r, c):
+        dd, hs, m = plans[c]
+        if r in dd:
+            return dd.index(r)
+        return len(dd) + [ds.index(r) for h, ds in hs if r in ds][0]
 
     def work(r):
-        return [r] + sorted([c for c in range(NR) if c != r], key=lambda c: (targets(c).index(r), (r - c) % NR))
+        o = sorted([c for c in range(NR) if c != r], key=lambda c: (step(r, c), (r - c) % NR))
+        o.insert(O["ownpos"], r)
+        return o
+    sent = [0]
+
+    def send(out, src, sem, d, m=None):
+        rid, pid, _ = topo.addr(d)
+        m = m or topo.mask(core, d)
+        g.remote_dma(out, src, sem, T.sem.sent, pid, rid, m)
+        sent[0] += bits(m)
+    if me is None:
+        for c, ds in helps:
+            a, b = off[c], off[c] + wid[c]
+            codes, plane = T.xq[:, a:b].bitcast(dt.uint8), T.xs[:, a:b]
+            g.wait_ge(T.sem["x%d" % c], 2 * bits(plans[c][2]))
+            for r in ds:
+                send(codes, codes, T.sem["x%d" % c], cores[r])
+                send(plane, plane, T.sem["x%d" % c], cores[r])
+        g.wait_ge(T.sem.sent, sent[0])
+        return
     order = work(me)
     W = wid[me]
     S, V, E = g.scalar, g.vector, g.tensor
-    sent = [0]
-
-    def send(out, src, sem, d):
-        rid, pid, _ = topo.addr(d)
-        m = topo.mask(core, d)
-        g.remote_dma(out, src, sem, T.sem.sent, pid, rid, m)
-        sent[0] += bits(m)
     g.sync.dma_start(T.xb[:, :4 * W], T.x[:, :4 * W]).then_inc(T.sem.lx, 16)
     for i in range(4):
         g.sync.dma_start(T.w1b[:, 512 * i:512 * i + 512], T.w1[:, 512 * i:512 * i + 512]).then_inc(T.sem["lw%d" % i], 16)
@@ -68,9 +95,12 @@ def rank_program(g, core, T, topo):
         V.quantize_mx(T.wq[:, 128 * i:128 * i + 128], T.ws[:, 128 * i:128 * i + 128], src).then_inc(T.sem.qw, 1)
     g.wait_ge(T.sem.qx, 1)
     codes, plane = T.xq[:, a:b].bitcast(dt.uint8), T.xs[:, a:b]
-    for r in targets(me):
-        send(codes, codes, T.sem["x%d" % me], cores[r])
-        send(plane, plane, T.sem["x%d" % me], cores[r])
+    dd, hs, hm = plans[me]
+    L = [(cores[r], None) for r in dd]
+    L[O["hpos"]:O["hpos"]] = [(h, hm) for h, ds in hs]
+    for d, m in L:
+        send(codes, codes, T.sem["x%d" % me], d, m)
+        send(plane, plane, T.sem["x%d" % me], d, m)
 
     vb, sb, ring = (1, 3), (0, 2), 6
 
@@ -123,10 +153,14 @@ def rank_program(g, core, T, topo):
 
     first(0)
     for k in range(1, NR):
-        first(k)
-        second(k - 1)
+        if k in O["np"]:
+            second(k - 1)
+            first(k)
+        else:
+            first(k)
+            second(k - 1)
     second(NR - 1)
-    V.wait_ge(T.sem.ev, 1)
+    V.wait_ge(T.sem.ev, order.index(me) + 1)
     senders = sorted([r for r in range(NR) if r != me], key=lambda r: (work(r).index(me), (r - me) % NR))
     prev = T.yo[:, a:a + W]
     for i, r in enumerate(senders):

from concourse.bass import DstId, RemoteDMATransfer
from concourse.mybir import dt, AluOpType, ActivationFunctionType

NR = 7
TOT = 1152
CFG = {"nd": 4, "nh": 1, "hpos": 1, "ownpos": 0, "np": ()}
OPT = {}

SCRATCH = {
    "xb": ("sbuf", [128, 768], "bfloat16"),
    "w1b": ("sbuf", [128, 2048], "bfloat16"),
    "w2b": ("sbuf", [128, 512], "bfloat16"),
    "xq": ("sbuf", [128, TOT], "float8_e4m3fn_x4"),
    "xs": ("sbuf", [128, TOT], "uint8"),
    "wq": ("sbuf", [128, 640], "float8_e4m3fn_x4"),
    "ws": ("sbuf", [128, 640], "uint8"),
    "h": ("sbuf", [128, 4 * TOT], "bfloat16"),
    "hq": ("sbuf", [128, TOT], "float8_e4m3fn_x4"),
    "hs": ("sbuf", [128, TOT], "uint8"),
    "yo": ("sbuf", [128, TOT], "float32"),
    "yl": ("sbuf", [128, NR * 192], "float32"),
    "acc": ("sbuf", [128, 192], "float32"),
    "pz": ("psum", [128, 512 * 6], "float32"),
    "py": ("psum", [128, 512 * 2], "float32"),
}
SEMAPHORES = (["lx", "lw0", "lw1", "lw2", "lw3", "lw4", "qx", "qw", "z", "rs", "rv", "qh", "ym", "ev", "sent", "ac", "st"]
              + ["x%d" % c for c in range(NR)] + ["y%d" % r for r in range(NR)])


def bits(m):
    return bin(m).count("1")


def rank_program(g, core, T, topo):
    O = dict(CFG)
    O.update(OPT)
    me = T.rank_of(core)
    cores = list(T.cores)
    wid = T.tables["WID"]
    off = [sum(wid[:c]) for c in range(NR)]

    def plan(c):
        s = cores[c]
        rot = [(c + i) % NR for i in range(1, NR)]
        dd, hh = rot[:O["nd"]], rot[O["nd"]:]
        ok = [k for k in range(128) if k != s and topo.chip(k) == topo.chip(s) and all(topo.may_write(k, cores[r]) for r in rot)]
        hs = [k for k in ok if topo.die(k) != topo.die(s)][:O["nh"]]
        out, on = topo.mask(s, cores[rot[0]]), topo.mask(s, ok[0])
        return dd, [(h, hh[j::len(hs)]) for j, h in enumerate(hs)], on & ~out
    plans = [plan(c) for c in range(NR)]
    helps = [(c, ds) for c in range(NR) for h, ds in plans[c][1] if h == core]
    if me is None and not helps:
        return

    def step(r, c):
        dd, hs, m = plans[c]
        if r in dd:
            return dd.index(r)
        return len(dd) + [ds.index(r) for h, ds in hs if r in ds][0]

    def work(r):
        o = sorted([c for c in range(NR) if c != r], key=lambda c: (step(r, c), (r - c) % NR))
        o.insert(O["ownpos"], r)
        return o
    sent = [0]

    def send(out, src, sem, d, m=None):
        rid, pid, _ = topo.addr(d)
        m = m or topo.mask(core, d)
        g.remote_dma(out, src, sem, T.sem.sent, pid, rid, m)
        sent[0] += bits(m)
    if me is None:
        for c, ds in helps:
            a, b = off[c], off[c] + wid[c]
            codes, plane = T.xq[:, a:b].bitcast(dt.uint8), T.xs[:, a:b]
            g.wait_ge(T.sem["x%d" % c], 2 * bits(plans[c][2]))
            for r in ds:
                send(codes, codes, T.sem["x%d" % c], cores[r])
                send(plane, plane, T.sem["x%d" % c], cores[r])
        g.wait_ge(T.sem.sent, sent[0])
        return
    order = work(me)
    W = wid[me]
    S, V, E = g.scalar, g.vector, g.tensor
    g.sync.dma_start(T.xb[:, :4 * W], T.x[:, :4 * W]).then_inc(T.sem.lx, 16)
    for i in range(4):
        g.sync.dma_start(T.w1b[:, 512 * i:512 * i + 512], T.w1[:, 512 * i:512 * i + 512]).then_inc(T.sem["lw%d" % i], 16)
    g.sync.dma_start(T.w2b[:], T.w2[:]).then_inc(T.sem.lw4, 16)
    a, b = off[me], off[me] + W
    V.wait_ge(T.sem.lx, 16)
    V.quantize_mx(T.xq[:, a:b], T.xs[:, a:b], T.xb[:, :4 * W]).then_inc(T.sem.qx, 1)
    for i in range(5):
        V.wait_ge(T.sem["lw%d" % i], 16)
        src = T.w1b[:, 512 * i:512 * i + 512] if i < 4 else T.w2b[:]
        V.quantize_mx(T.wq[:, 128 * i:128 * i + 128], T.ws[:, 128 * i:128 * i + 128], src).then_inc(T.sem.qw, 1)
    g.wait_ge(T.sem.qx, 1)
    codes, plane = T.xq[:, a:b].bitcast(dt.uint8), T.xs[:, a:b]
    dd, hs, hm = plans[me]
    L = [(cores[r], None) for r in dd]
    L[O["hpos"]:O["hpos"]] = [(h, hm) for h, ds in hs]
    for d, m in L:
        send(codes, codes, T.sem["x%d" % me], d, m)
        send(plane, plane, T.sem["x%d" % me], d, m)

    vb, sb, ring = (1, 3), (0, 2), 6

    def left(m):
        return (T.sem.rv if m % 4 in vb else T.sem.rs), m // 4 * 2 + m % 4 // 2 + 1

    def first(k):
        c = order[k]
        n, a = wid[c], off[c]
        if c == me:
            E.wait_ge(T.sem.qx, 1)
        else:
            E.wait_ge(T.sem["x%d" % c], 2 * bits(topo.mask(cores[c], core)))
        for b in range(4):
            m = 4 * k + b
            if k == 0:
                E.wait_ge(T.sem.qw, b + 1)
            if m >= ring:
                E.wait_ge(*left(m - ring))
            p = 512 * (m % ring)
            E.matmul_mx(T.pz[:, p:p + n], T.wq[:, 128 * b:128 * b + 128], T.ws[:, 128 * b:128 * b + 128],
                        T.xq[:, a:a + n], T.xs[:, a:a + n], True, True).then_inc(T.sem.z, 1)
            out = T.h[:, 4 * a + b:4 * (a + n):4]
            if b in vb:
                V.wait_ge(T.sem.z, m + 1)
                V.tensor_scalar(out, T.pz[:, p:p + n], 0.0, 0.043, AluOpType.max, AluOpType.mult).then_inc(T.sem.rv, 1)
            else:
                S.wait_ge(T.sem.z, m + 1)
                S.activation(out, T.pz[:, p:p + n], ActivationFunctionType.Relu, scale=0.043).then_inc(T.sem.rs, 1)
        V.wait_ge(T.sem.rs, 2 * (k + 1))
        V.wait_ge(T.sem.rv, 2 * (k + 1))
        V.quantize_mx(T.hq[:, a:a + n], T.hs[:, a:a + n], T.h[:, 4 * a:4 * (a + n)]).then_inc(T.sem.qh, 1)

    def second(k):
        c = order[k]
        n, a = wid[c], off[c]
        if k == 0:
            E.wait_ge(T.sem.qw, 5)
        E.wait_ge(T.sem.qh, k + 1)
        if k >= 2:
            E.wait_ge(T.sem.ev, k - 1)
        p = 512 * (k % 2)
        E.matmul_mx(T.py[:, p:p + n], T.wq[:, 512:640], T.ws[:, 512:640], T.hq[:, a:a + n], T.hs[:, a:a + n],
                    True, True).then_inc(T.sem.ym, 1)
        S.wait_ge(T.sem.ym, k + 1)
        S.activation(T.yo[:, a:a + n], T.py[:, p:p + n], ActivationFunctionType.Copy).then_inc(T.sem.ev, 1)
        if c != me:
            g.wait_ge(T.sem.ev, k + 1)
            send(T.yl[:, 192 * me:192 * me + n], T.yo[:, a:a + n], T.sem["y%d" % me], cores[c])

    first(0)
    for k in range(1, NR):
        if k in O["np"]:
            second(k - 1)
            first(k)
        else:
            first(k)
            second(k - 1)
    second(NR - 1)
    V.wait_ge(T.sem.ev, order.index(me) + 1)
    senders = sorted([r for r in range(NR) if r != me], key=lambda r: (work(r).index(me), (r - me) % NR))
    prev = T.yo[:, a:a + W]
    for i, r in enumerate(senders):
        V.wait_ge(T.sem["y%d" % r], bits(topo.mask(cores[r], core)))
        if i:
            V.wait_ge(T.sem.ac, i)
        V.tensor_tensor(T.acc[:, :W], prev, T.yl[:, 192 * r:192 * r + W], AluOpType.add).then_inc(T.sem.ac, 1)
        prev = T.acc[:, :W]
    g.sync.wait_ge(T.sem.ac, len(senders))
    g.sync.dma_start(T.y[:, :W], T.acc[:, :W]).then_inc(T.sem.st, 16)
    g.sync.wait_ge(T.sem.st, 16)
    g.wait_ge(T.sem.sent, sent[0])
